import numpy as np, ml_dtypes
CORES = [8,80,112,136,208,240,264,336,368,392,464,496]
N = 12
GR, GC, HH, WW = 4, 3, 8, 16
def setup_inputs(rng):
    return {"x": rng.standard_normal((N, 128, HH * WW), dtype=np.float32).astype(ml_dtypes.bfloat16), "w": rng.standard_normal((N, 128, 9 * 128), dtype=np.float32).astype(ml_dtypes.bfloat16)}
def setup_inputs_big(rng):
    d = setup_inputs(rng)
    for k in ("x", "w"): d[k] = (d[k].astype(np.float32) * 1024.0).astype(d[k].dtype)
    return d
def setup_inputs_small(rng):
    d = setup_inputs(rng)
    for k in ("x", "w"): d[k] = (d[k].astype(np.float32) * (1 / 1024.0)).astype(d[k].dtype)
    return d
def setup_inputs_apart(rng):
    d = setup_inputs(rng)
    f = (10.0 ** rng.permutation(np.linspace(-1.5, 1.5, N))).astype(np.float32).reshape(N, 1, 1)
    for k in ("x", "w"): d[k] = (d[k].astype(np.float32) * f).astype(d[k].dtype)
    return d
def reference(x, w):
    X = x.astype(np.float64).reshape(GR, GC, 128, HH, WW); W = w.astype(np.float64)
    g = np.concatenate([np.concatenate(list(X[i]), axis=2) for i in range(GR)], axis=1)
    y = np.zeros((N, 128, HH * WW))
    for r in range(N):
        i0, j0 = HH * (r // GC), WW * (r % GC)
        for a in range(3):
            for b in range(3):
                sh = np.roll(g, (-2 * (a - 1), -2 * (b - 1)), axis=(1, 2))[:, i0:i0 + HH, j0:j0 + WW]
                y[r] += W[r][:, 128 * (3 * a + b):128 * (3 * a + b) + 128].T @ sh.reshape(128, HH * WW)
    return {"y": y.astype(ml_dtypes.bfloat16 if x.dtype != np.float64 else np.float64)}

@@ -1,0 +1,143 @@
+from concourse.bass import DstId, RemoteDMATransfer
+
+GR, GC, HH, WW = 4, 3, 8, 16
+HP = WW // 2
+
+E_HOP1 = 4
+E_HOP2 = 8
+E_VERT = 4
+
+SCRATCH = {
+    "xs": ("sbuf", [128, HH, HP, 2], "bfloat16"),
+    "wsb": ("sbuf", [128, 9 * 128], "bfloat16"),
+    "lr": ("sbuf", [128, 2, HH, 2], "bfloat16"),
+    "strip": ("sbuf", [128, HH, 2], "bfloat16"),
+    "vert": ("sbuf", [128, 2, 2, HP, 2], "bfloat16"),
+    "tall": ("sbuf", [128, 2, 3 * HH, 2], "bfloat16"),
+    "ysb": ("sbuf", [128, HH, HP, 2], "bfloat16"),
+    "ps": ("psum", [128, HH, HP, 2], "float32"),
+}
+SEMAPHORES = ["xld", "wld", "packed", "hin", "vert", "horiz", "sent", "mm", "evac", "yst"]
+
+_CACHE = {}
+
+
+def _plan(T, topo):
+    if "plan" in _CACHE:
+        return _CACHE["plan"]
+    cores = list(T.cores)
+    world = range((1 + max(topo.host(c) for c in cores)) * topo.CORES_PER_HOST)
+    by_rank, by_helper = {}, {}
+    for r, me in enumerate(cores):
+        row, col = divmod(r, GC)
+        dests = [[(cores[((row + dh) % GR) * GC + (col + s) % GC], 1 - dh) for dh in (-1, 0, 1)] for s in (-1, 1)]
+        every = [d for side in dests for d, _ in side]
+        cand = [k for k in world
+                if topo.host(k) == topo.host(me) and topo.chip(k) == topo.chip(me) and k not in cores
+                and all(topo.may_write(k, d) for d in every)]
+        cand.sort(key=lambda k: (topo.die(k) != topo.die(me), k))
+        by_rank[r] = cand[:2]
+        for side in (0, 1):
+            by_helper[cand[side]] = (side, dests[side])
+    _CACHE["plan"] = (by_rank, by_helper)
+    return _CACHE["plan"]
+
+
+def _engines(topo, src, dsts):
+    m = topo.mask(src, dsts[0])
+    for d in dsts[1:]:
+        m &= topo.mask(src, d)
+    return [e for e in range(m.bit_length()) if (m >> e) & 1]
+
+
+def _mask(engines):
+    return sum(1 << e for e in engines)
+
+
+def _dst(topo, d, src):
+    rid, pid = topo.addr(d, src)
+    return DstId(rid=rid, pnc=pid)
+
+
+def _helper(g, core, T, topo, side, dests):
+    eng = _engines(topo, core, [d for d, _ in dests])[:E_HOP2]
+    g.wait_ge(T.sem.hin, E_HOP1)
+    g.remote_dma_fused([RemoteDMATransfer(
+        dst_ids=[_dst(topo, d, core) for d, _ in dests],
+        dma_engine_mask=_mask(eng),
+        remote_sem=T.sem.horiz,
+        srcs=[T.strip[:]],
+        dsts=[T.tall[:, 1 - side, HH * blk:HH * blk + HH, :] for _, blk in dests],
+        alu_op=0)], local_sem=T.sem.sent)
+    g.wait_ge(T.sem.sent, E_HOP2)
+
+
+def rank_program(g, core, T, topo):
+    by_rank, by_helper = _plan(T, topo)
+    rank = T.rank_of(core)
+    if rank is None:
+        if core in by_helper:
+            _helper(g, core, T, topo, *by_helper[core])
+        return
+    sem = T.sem
+    cores = list(T.cores)
+    row, col = divmod(rank, GC)
+    up, down = cores[((row - 1) % GR) * GC + col], cores[((row + 1) % GR) * GC + col]
+    helpers = by_rank[rank]
+
+    g.sync.dma_start(T.xs[:], T.x[:]).then_inc(sem.xld, 16)
+    g.sync.dma_start(T.wsb[:], T.w[:]).then_inc(sem.wld, 16)
+
+    g.vector.wait_ge(sem.xld, 16)
+    g.vector.tensor_copy(T.lr[:, 0], T.xs[:, :, 0, :]).then_inc(sem.packed, 1)
+    g.vector.tensor_copy(T.lr[:, 1], T.xs[:, :, HP - 1, :]).then_inc(sem.packed, 1)
+
+    eng = _engines(topo, core, helpers + [up, down])
+    g.wait_ge(sem.packed, 2)
+    g.remote_dma_fused([RemoteDMATransfer(
+        dst_ids=[_dst(topo, helpers[s], core)],
+        dma_engine_mask=_mask(eng[s * E_HOP1:(s + 1) * E_HOP1]),
+        remote_sem=sem.hin, srcs=[T.lr[:, s]], dsts=[T.strip[:]], alu_op=0) for s in (0, 1)], local_sem=sem.sent)
+    g.wait_ge(sem.xld, 16)
+    g.remote_dma_fused([
+        RemoteDMATransfer(dst_ids=[_dst(topo, up, core)], dma_engine_mask=_mask(eng[0:E_VERT]),
+                          remote_sem=sem.vert, srcs=[T.xs[:, 0:2]], dsts=[T.vert[:, 1]], alu_op=0),
+        RemoteDMATransfer(dst_ids=[_dst(topo, down, core)], dma_engine_mask=_mask(eng[E_VERT:2 * E_VERT]),
+                          remote_sem=sem.vert, srcs=[T.xs[:, HH - 2:HH]], dsts=[T.vert[:, 0]], alu_op=0),
+    ], local_sem=sem.sent)
+
+    def span(shift, n):
+        return max(0, -shift), min(n, n - shift)
+
+    own, rows, columns = [], [], []
+    for a, b in [(1, 1)] + [(a, b) for a in range(3) for b in range(3) if (a, b) != (1, 1)]:
+        di, pj = 2 * (a - 1), b - 1
+        i0, i1 = span(di, HH)
+        p0, p1 = span(pj, HP)
+        own.append((T.ps[:, i0:i1, p0:p1, :], a, b, T.xs[:, i0 + di:i1 + di, p0 + pj:p1 + pj, :]))
+        if a == 0:
+            rows.append((T.ps[:, 0:2, p0:p1, :], a, b, T.vert[:, 0, :, p0 + pj:p1 + pj, :]))
+        if a == 2:
+            rows.append((T.ps[:, HH - 2:HH, p0:p1, :], a, b, T.vert[:, 1, :, p0 + pj:p1 + pj, :]))
+        if b == 0:
+            columns.append((T.ps[:, :, 0, :], a, b, T.tall[:, 0, HH + di:2 * HH + di, :]))
+        if b == 2:
+            columns.append((T.ps[:, :, HP - 1, :], a, b, T.tall[:, 1, HH + di:2 * HH + di, :]))
+    total = len(own) + len(rows) + len(columns)
+    done = 0
+    for waits, batch in (([(sem.xld, 16), (sem.wld, 16)], own),
+                         ([(sem.vert, 2 * E_VERT)], rows),
+                         ([(sem.horiz, 6 * E_HOP2)], columns)):
+        for s, n in waits:
+            g.tensor.wait_ge(s, n)
+        for out, a, b, rhs in batch:
+            k = 128 * (3 * a + b)
+            done += 1
+            g.tensor.matmul(out, T.wsb[:, k:k + 128], rhs, start=(done == 1), stop=(done == total)).then_inc(sem.mm, 1)
+
+    g.vector.wait_ge(sem.mm, total)
+    g.vector.tensor_copy(T.ysb[:], T.ps[:]).then_inc(sem.evac, 1)
+    g.sync.wait_ge(sem.evac, 1)
+    g.sync.dma_start(T.y[:], T.ysb[:]).then_inc(sem.yst, 16)
+    g.wait_ge(sem.sent, 2 * E_HOP1 + 2 * E_VERT)
+    g.wait_ge(sem.yst, 16)

@@ -1,23 +1,29 @@
 from concourse.bass import DstId, RemoteDMATransfer
+from concourse.mybir import AluOpType, ActivationFunctionType
 
 GR, GC, HH, WW = 4, 3, 8, 16
 HP = WW // 2
+BANK = 512
 
-E_HOP1 = 4
+E_HOP1 = 8
 E_HOP2 = 8
-E_VERT = 4
+E_VERT = 2
 
 SCRATCH = {
     "xs": ("sbuf", [128, HH, HP, 2], "bfloat16"),
     "wsb": ("sbuf", [128, 9 * 128], "bfloat16"),
     "lr": ("sbuf", [128, 2, HH, 2], "bfloat16"),
-    "strip": ("sbuf", [128, HH, 2], "bfloat16"),
+    "strips": ("sbuf", [128, 2, HH, 2], "bfloat16"),
     "vert": ("sbuf", [128, 2, 2, HP, 2], "bfloat16"),
     "tall": ("sbuf", [128, 2, 3 * HH, 2], "bfloat16"),
+    "edge": ("sbuf", [128, 2, HH, 2], "float32"),
     "ysb": ("sbuf", [128, HH, HP, 2], "bfloat16"),
-    "ps": ("psum", [128, HH, HP, 2], "float32"),
+    "psa": ("psum", [128, BANK // (2 * HP), HP, 2], "float32"),
+    "pss0": ("psum", [128, BANK // 2, 2], "float32"),
+    "pss1": ("psum", [128, BANK // 2, 2], "float32"),
 }
-SEMAPHORES = ["xld", "wld", "packed", "hin", "vert", "horiz", "sent", "mm", "evac", "yst"]
+SEMAPHORES = (["xld", "wld", "packed", "hin", "vert", "sent", "mma", "mms0", "mms1", "eva", "evs", "yst"]
+              + ["hz%d%d" % (r, t) for r in range(GR) for t in (0, 1)])
 
 _CACHE = {}
 
@@ -38,9 +44,15 @@ def _plan(T, topo):
         cand.sort(key=lambda k: (topo.die(k) != topo.die(me), k))
         by_rank[r] = cand[:2]
         for side in (0, 1):
-            by_helper[cand[side]] = (side, dests[side])
+            by_helper[cand[side]] = (side, row, sorted(dests[side], key=lambda db: _far(topo, me, db[0])))
     _CACHE["plan"] = (by_rank, by_helper)
     return _CACHE["plan"]
+
+
+def _far(topo, a, b):
+    if topo.rack(topo.host(a)) != topo.rack(topo.host(b)):
+        return 0
+    return 1 if topo.host(a) == topo.host(b) else 2
 
 
 def _engines(topo, src, dsts):
@@ -59,14 +71,14 @@ def _dst(topo, d, src):
     return DstId(rid=rid, pnc=pid)
 
 
-def _helper(g, core, T, topo, side, dests):
+def _helper(g, core, T, topo, side, row, dests):
     eng = _engines(topo, core, [d for d, _ in dests])[:E_HOP2]
     g.wait_ge(T.sem.hin, E_HOP1)
     g.remote_dma_fused([RemoteDMATransfer(
         dst_ids=[_dst(topo, d, core) for d, _ in dests],
         dma_engine_mask=_mask(eng),
-        remote_sem=T.sem.horiz,
-        srcs=[T.strip[:]],
+        remote_sem=T.sem["hz%d%d" % (row, 1 - side)],
+        srcs=[T.strips[:, side]],
         dsts=[T.tall[:, 1 - side, HH * blk:HH * blk + HH, :] for _, blk in dests],
         alu_op=0)], local_sem=T.sem.sent)
     g.wait_ge(T.sem.sent, E_HOP2)
@@ -90,54 +102,75 @@ def rank_program(g, core, T, topo):
 
     g.vector.wait_ge(sem.xld, 16)
     g.vector.tensor_copy(T.lr[:, 0], T.xs[:, :, 0, :]).then_inc(sem.packed, 1)
-    g.vector.tensor_copy(T.lr[:, 1], T.xs[:, :, HP - 1, :]).then_inc(sem.packed, 1)
+    g.scalar.wait_ge(sem.xld, 16)
+    g.scalar.activation(T.lr[:, 1], T.xs[:, :, HP - 1, :], ActivationFunctionType.Copy).then_inc(sem.packed, 1)
 
-    eng = _engines(topo, core, helpers + [up, down])
-    g.wait_ge(sem.packed, 2)
-    g.remote_dma_fused([RemoteDMATransfer(
-        dst_ids=[_dst(topo, helpers[s], core)],
-        dma_engine_mask=_mask(eng[s * E_HOP1:(s + 1) * E_HOP1]),
-        remote_sem=sem.hin, srcs=[T.lr[:, s]], dsts=[T.strip[:]], alu_op=0) for s in (0, 1)], local_sem=sem.sent)
+    off = _engines(topo, core, [up, down])[:2 * E_VERT]
+    on = [e for e in _engines(topo, core, helpers) if e not in off][:E_HOP1]
     g.wait_ge(sem.xld, 16)
     g.remote_dma_fused([
-        RemoteDMATransfer(dst_ids=[_dst(topo, up, core)], dma_engine_mask=_mask(eng[0:E_VERT]),
+        RemoteDMATransfer(dst_ids=[_dst(topo, up, core)], dma_engine_mask=_mask(off[0:E_VERT]),
                           remote_sem=sem.vert, srcs=[T.xs[:, 0:2]], dsts=[T.vert[:, 1]], alu_op=0),
-        RemoteDMATransfer(dst_ids=[_dst(topo, down, core)], dma_engine_mask=_mask(eng[E_VERT:2 * E_VERT]),
+        RemoteDMATransfer(dst_ids=[_dst(topo, down, core)], dma_engine_mask=_mask(off[E_VERT:2 * E_VERT]),
                           remote_sem=sem.vert, srcs=[T.xs[:, HH - 2:HH]], dsts=[T.vert[:, 0]], alu_op=0),
     ], local_sem=sem.sent)
+    g.wait_ge(sem.packed, 2)
+    g.remote_dma_fused([RemoteDMATransfer(
+        dst_ids=[_dst(topo, h, core) for h in helpers], dma_engine_mask=_mask(on),
+        remote_sem=sem.hin, srcs=[T.lr[:]], dsts=[T.strips[:] for h in helpers], alu_op=0)], local_sem=sem.sent)
 
     def span(shift, n):
         return max(0, -shift), min(n, n - shift)
 
-    own, rows, columns = [], [], []
+    def lhs(a, b):
+        k = 128 * (3 * a + b)
+        return T.wsb[:, k:k + 128]
+
+    own, rows = [], []
     for a, b in [(1, 1)] + [(a, b) for a in range(3) for b in range(3) if (a, b) != (1, 1)]:
         di, pj = 2 * (a - 1), b - 1
         i0, i1 = span(di, HH)
         p0, p1 = span(pj, HP)
-        own.append((T.ps[:, i0:i1, p0:p1, :], a, b, T.xs[:, i0 + di:i1 + di, p0 + pj:p1 + pj, :]))
+        own.append((T.psa[:, i0:i1, p0:p1, :], a, b, T.xs[:, i0 + di:i1 + di, p0 + pj:p1 + pj, :]))
         if a == 0:
-            rows.append((T.ps[:, 0:2, p0:p1, :], a, b, T.vert[:, 0, :, p0 + pj:p1 + pj, :]))
+            rows.append((T.psa[:, 0:2, p0:p1, :], a, b, T.vert[:, 0, :, p0 + pj:p1 + pj, :]))
         if a == 2:
-            rows.append((T.ps[:, HH - 2:HH, p0:p1, :], a, b, T.vert[:, 1, :, p0 + pj:p1 + pj, :]))
-        if b == 0:
-            columns.append((T.ps[:, :, 0, :], a, b, T.tall[:, 0, HH + di:2 * HH + di, :]))
-        if b == 2:
-            columns.append((T.ps[:, :, HP - 1, :], a, b, T.tall[:, 1, HH + di:2 * HH + di, :]))
-    total = len(own) + len(rows) + len(columns)
+            rows.append((T.psa[:, HH - 2:HH, p0:p1, :], a, b, T.vert[:, 1, :, p0 + pj:p1 + pj, :]))
+    total = len(own) + len(rows)
     done = 0
-    for waits, batch in (([(sem.xld, 16), (sem.wld, 16)], own),
-                         ([(sem.vert, 2 * E_VERT)], rows),
-                         ([(sem.horiz, 6 * E_HOP2)], columns)):
+    for waits, batch in (([(sem.xld, 16), (sem.wld, 16)], own), ([(sem.vert, 2 * E_VERT)], rows)):
         for s, n in waits:
             g.tensor.wait_ge(s, n)
         for out, a, b, rhs in batch:
-            k = 128 * (3 * a + b)
             done += 1
-            g.tensor.matmul(out, T.wsb[:, k:k + 128], rhs, start=(done == 1), stop=(done == total)).then_inc(sem.mm, 1)
+            g.tensor.matmul(out, lhs(a, b), rhs, start=(done == 1), stop=(done == total)).then_inc(sem.mma, 1)
 
-    g.vector.wait_ge(sem.mm, total)
-    g.vector.tensor_copy(T.ysb[:], T.ps[:]).then_inc(sem.evac, 1)
-    g.sync.wait_ge(sem.evac, 1)
+    outer = sorted((0, 2), key=lambda a: _far(topo, core, cores[((row + a - 1) % GR) * GC + col]))
+    order = (1, 0)
+
+    def tap(t, a, first, last):
+        g.tensor.wait_ge(sem["hz%d%d" % ((row + a - 1) % GR, t)], E_HOP2)
+        di = 2 * (a - 1)
+        g.tensor.matmul(T["pss%d" % t][:, 0:HH, :], lhs(a, 2 * t), T.tall[:, t, HH + di:2 * HH + di, :],
+                        start=first, stop=last).then_inc(sem["mms%d" % t], 1)
+
+    for t in order:
+        tap(t, 1, True, False)
+        tap(t, outer[0], False, False)
+    for t in order:
+        tap(t, outer[1], False, True)
+
+    g.vector.wait_ge(sem.mma, total)
+    for t in (0, 1):
+        g.vector.tensor_copy(T.edge[:, t], T.psa[:, 0:HH, t * (HP - 1), :]).then_inc(sem.eva, 1)
+    g.vector.tensor_copy(T.ysb[:, :, 1:HP - 1, :], T.psa[:, 0:HH, 1:HP - 1, :]).then_inc(sem.eva, 1)
+    g.vector.wait_ge(sem.eva, 3)
+    for t in order:
+        g.vector.wait_ge(sem["mms%d" % t], 3)
+        g.vector.tensor_tensor(T.ysb[:, :, t * (HP - 1), :], T["pss%d" % t][:, 0:HH, :], T.edge[:, t],
+                               AluOpType.add).then_inc(sem.evs, 1)
+    g.sync.wait_ge(sem.eva, 3)
+    g.sync.wait_ge(sem.evs, 2)
     g.sync.dma_start(T.y[:], T.ysb[:]).then_inc(sem.yst, 16)
-    g.wait_ge(sem.sent, 2 * E_HOP1 + 2 * E_VERT)
+    g.wait_ge(sem.sent, E_HOP1 + 2 * E_VERT)
     g.wait_ge(sem.yst, 16)

from concourse.bass import DstId, RemoteDMATransfer
from concourse.mybir import AluOpType, ActivationFunctionType

GR, GC, HH, WW = 4, 3, 8, 16
HP = WW // 2
BANK = 512

E_HOP1 = 8
E_HOP2 = 8
E_VERT = 2

SCRATCH = {
    "xs": ("sbuf", [128, HH, HP, 2], "bfloat16"),
    "wsb": ("sbuf", [128, 9 * 128], "bfloat16"),
    "lr": ("sbuf", [128, 2, HH, 2], "bfloat16"),
    "strips": ("sbuf", [128, 2, HH, 2], "bfloat16"),
    "vert": ("sbuf", [128, 2, 2, HP, 2], "bfloat16"),
    "tall": ("sbuf", [128, 2, 3 * HH, 2], "bfloat16"),
    "edge": ("sbuf", [128, 2, HH, 2], "float32"),
    "ysb": ("sbuf", [128, HH, HP, 2], "bfloat16"),
    "psa": ("psum", [128, BANK // (2 * HP), HP, 2], "float32"),
    "pss0": ("psum", [128, BANK // 2, 2], "float32"),
    "pss1": ("psum", [128, BANK // 2, 2], "float32"),
}
SEMAPHORES = (["xld", "wld", "packed", "hin", "vert", "sent", "mma", "mms0", "mms1", "eva", "evs", "yst"]
              + ["hz%d%d" % (r, t) for r in range(GR) for t in (0, 1)])

_CACHE = {}


def _plan(T, topo):
    if "plan" in _CACHE:
        return _CACHE["plan"]
    cores = list(T.cores)
    world = range((1 + max(topo.host(c) for c in cores)) * topo.CORES_PER_HOST)
    by_rank, by_helper = {}, {}
    for r, me in enumerate(cores):
        row, col = divmod(r, GC)
        dests = [[(cores[((row + dh) % GR) * GC + (col + s) % GC], 1 - dh) for dh in (-1, 0, 1)] for s in (-1, 1)]
        every = [d for side in dests for d, _ in side]
        cand = [k for k in world
                if topo.host(k) == topo.host(me) and topo.chip(k) == topo.chip(me) and k not in cores
                and all(topo.may_write(k, d) for d in every)]
        cand.sort(key=lambda k: (topo.die(k) != topo.die(me), k))
        by_rank[r] = cand[:2]
        for side in (0, 1):
            by_helper[cand[side]] = (side, row, sorted(dests[side], key=lambda db: _far(topo, me, db[0])))
    _CACHE["plan"] = (by_rank, by_helper)
    return _CACHE["plan"]


def _far(topo, a, b):
    if topo.rack(topo.host(a)) != topo.rack(topo.host(b)):
        return 0
    return 1 if topo.host(a) == topo.host(b) else 2


def _engines(topo, src, dsts):
    m = topo.mask(src, dsts[0])
    for d in dsts[1:]:
        m &= topo.mask(src, d)
    return [e for e in range(m.bit_length()) if (m >> e) & 1]


def _mask(engines):
    return sum(1 << e for e in engines)


def _dst(topo, d, src):
    rid, pid = topo.addr(d, src)
    return DstId(rid=rid, pnc=pid)


def _helper(g, core, T, topo, side, row, dests):
    eng = _engines(topo, core, [d for d, _ in dests])[:E_HOP2]
    g.wait_ge(T.sem.hin, E_HOP1)
    g.remote_dma_fused([RemoteDMATransfer(
        dst_ids=[_dst(topo, d, core) for d, _ in dests],
        dma_engine_mask=_mask(eng),
        remote_sem=T.sem["hz%d%d" % (row, 1 - side)],
        srcs=[T.strips[:, side]],
        dsts=[T.tall[:, 1 - side, HH * blk:HH * blk + HH, :] for _, blk in dests],
        alu_op=0)], local_sem=T.sem.sent)
    g.wait_ge(T.sem.sent, E_HOP2)


def rank_program(g, core, T, topo):
    by_rank, by_helper = _plan(T, topo)
    rank = T.rank_of(core)
    if rank is None:
        if core in by_helper:
            _helper(g, core, T, topo, *by_helper[core])
        return
    sem = T.sem
    cores = list(T.cores)
    row, col = divmod(rank, GC)
    up, down = cores[((row - 1) % GR) * GC + col], cores[((row + 1) % GR) * GC + col]
    helpers = by_rank[rank]

    g.sync.dma_start(T.xs[:], T.x[:]).then_inc(sem.xld, 16)
    g.sync.dma_start(T.wsb[:], T.w[:]).then_inc(sem.wld, 16)

    g.vector.wait_ge(sem.xld, 16)
    g.vector.tensor_copy(T.lr[:, 0], T.xs[:, :, 0, :]).then_inc(sem.packed, 1)
    g.scalar.wait_ge(sem.xld, 16)
    g.scalar.activation(T.lr[:, 1], T.xs[:, :, HP - 1, :], ActivationFunctionType.Copy).then_inc(sem.packed, 1)

    off = _engines(topo, core, [up, down])[:2 * E_VERT]
    on = [e for e in _engines(topo, core, helpers) if e not in off][:E_HOP1]
    g.wait_ge(sem.xld, 16)
    g.remote_dma_fused([
        RemoteDMATransfer(dst_ids=[_dst(topo, up, core)], dma_engine_mask=_mask(off[0:E_VERT]),
                          remote_sem=sem.vert, srcs=[T.xs[:, 0:2]], dsts=[T.vert[:, 1]], alu_op=0),
        RemoteDMATransfer(dst_ids=[_dst(topo, down, core)], dma_engine_mask=_mask(off[E_VERT:2 * E_VERT]),
                          remote_sem=sem.vert, srcs=[T.xs[:, HH - 2:HH]], dsts=[T.vert[:, 0]], alu_op=0),
    ], local_sem=sem.sent)
    g.wait_ge(sem.packed, 2)
    g.remote_dma_fused([RemoteDMATransfer(
        dst_ids=[_dst(topo, h, core) for h in helpers], dma_engine_mask=_mask(on),
        remote_sem=sem.hin, srcs=[T.lr[:]], dsts=[T.strips[:] for h in helpers], alu_op=0)], local_sem=sem.sent)

    def span(shift, n):
        return max(0, -shift), min(n, n - shift)

    def lhs(a, b):
        k = 128 * (3 * a + b)
        return T.wsb[:, k:k + 128]

    own, rows = [], []
    for a, b in [(1, 1)] + [(a, b) for a in range(3) for b in range(3) if (a, b) != (1, 1)]:
        di, pj = 2 * (a - 1), b - 1
        i0, i1 = span(di, HH)
        p0, p1 = span(pj, HP)
        own.append((T.psa[:, i0:i1, p0:p1, :], a, b, T.xs[:, i0 + di:i1 + di, p0 + pj:p1 + pj, :]))
        if a == 0:
            rows.append((T.psa[:, 0:2, p0:p1, :], a, b, T.vert[:, 0, :, p0 + pj:p1 + pj, :]))
        if a == 2:
            rows.append((T.psa[:, HH - 2:HH, p0:p1, :], a, b, T.vert[:, 1, :, p0 + pj:p1 + pj, :]))
    total = len(own) + len(rows)
    done = 0
    for waits, batch in (([(sem.xld, 16), (sem.wld, 16)], own), ([(sem.vert, 2 * E_VERT)], rows)):
        for s, n in waits:
            g.tensor.wait_ge(s, n)
        for out, a, b, rhs in batch:
            done += 1
            g.tensor.matmul(out, lhs(a, b), rhs, start=(done == 1), stop=(done == total)).then_inc(sem.mma, 1)

    outer = sorted((0, 2), key=lambda a: _far(topo, core, cores[((row + a - 1) % GR) * GC + col]))
    order = (1, 0)

    def tap(t, a, first, last):
        g.tensor.wait_ge(sem["hz%d%d" % ((row + a - 1) % GR, t)], E_HOP2)
        di = 2 * (a - 1)
        g.tensor.matmul(T["pss%d" % t][:, 0:HH, :], lhs(a, 2 * t), T.tall[:, t, HH + di:2 * HH + di, :],
                        start=first, stop=last).then_inc(sem["mms%d" % t], 1)

    for t in order:
        tap(t, 1, True, False)
        tap(t, outer[0], False, False)
    for t in order:
        tap(t, outer[1], False, True)

    g.vector.wait_ge(sem.mma, total)
    for t in (0, 1):
        g.vector.tensor_copy(T.edge[:, t], T.psa[:, 0:HH, t * (HP - 1), :]).then_inc(sem.eva, 1)
    g.vector.tensor_copy(T.ysb[:, :, 1:HP - 1, :], T.psa[:, 0:HH, 1:HP - 1, :]).then_inc(sem.eva, 1)
    g.vector.wait_ge(sem.eva, 3)
    for t in order:
        g.vector.wait_ge(sem["mms%d" % t], 3)
        g.vector.tensor_tensor(T.ysb[:, :, t * (HP - 1), :], T["pss%d" % t][:, 0:HH, :], T.edge[:, t],
                               AluOpType.add).then_inc(sem.evs, 1)
    g.sync.wait_ge(sem.eva, 3)
    g.sync.wait_ge(sem.evs, 2)
    g.sync.dma_start(T.y[:], T.ysb[:]).then_inc(sem.yst, 16)
    g.wait_ge(sem.sent, E_HOP1 + 2 * E_VERT)
    g.wait_ge(sem.yst, 16)
